import numpy as np
import ml_dtypes


def mxq(x, axis, fmt="e4m3"):
    dtype, down = {"e4m3": (ml_dtypes.float8_e4m3fn, 7), "e5m2": (ml_dtypes.float8_e5m2, 14)}[fmt]
    v = np.moveaxis(np.asarray(x, np.float32).astype(ml_dtypes.bfloat16).astype(np.float64), axis, -1)
    blocks = v.reshape(v.shape[:-1] + (-1, 32))
    amax = np.abs(blocks).max(-1, keepdims=True)
    byte = np.maximum(np.where(amax > 0, np.frexp(amax)[1] - 1 + 127, 0) - down, 1)
    scale = np.exp2(byte - 127.0)
    codes = (blocks / scale).astype(np.float32).astype(dtype).astype(np.float64)
    return np.moveaxis((codes * scale).reshape(v.shape), -1, axis)


WIDE = False


def mx_kscale(k):
    if not WIDE:
        return np.ones(k)
    levels = np.array([10, -10, 5, -5, 0])
    if k % 512:
        return np.exp2(np.random.permutation(np.resize(levels, k // 32))).repeat(32)
    a = np.empty((k // 512, 16))
    for p in range(k // 512):
        a[p, :8] = np.random.permutation(np.resize(levels, 8))
        for g in range(8):
            far = levels[np.abs(levels - a[p, g]) >= 10]
            a[p, g + 8] = far[np.random.randint(len(far))]
    return np.exp2(a.ravel()).repeat(32)


def f64(x):
    return np.asarray(x).astype(np.float64)


def striped8(idx):
    return np.asarray(idx).reshape(8, -1, 16).transpose(0, 2, 1).reshape(128, -1).astype(np.uint16)


def unstriped8(offs):
    return offs.reshape(8, 16, -1).transpose(0, 2, 1).reshape(8, -1).astype(np.int64)


def pick8(x, idx, run):
    r = np.arange(len(x))
    return x[r[:, None], idx[r % (8 * run) // run]]


E2M1 = np.array([0.0, 0.5, 1.0, 1.5, 2.0, 3.0, 4.0, 6.0, -0.0, -0.5, -1.0, -1.5, -2.0, -3.0, -4.0, -6.0])


def pack_weight(w, fmt):
    k, n = w.shape
    w = f64(np.asarray(w, np.float32).astype(ml_dtypes.bfloat16)).reshape(k // 32, 32, n)
    amax = np.abs(w).max(1)
    if fmt == "e4m3":
        byte = np.frexp(amax)[1] - 1 + 127 - 7
    else:
        mant, ex = np.frexp(amax / 6.0)
        byte = np.where(mant > 0.5, ex, ex - 1) + 127
    byte = np.clip(np.where(amax > 0, byte, 1), 1, 254)
    scaled = (w * np.exp2(127.0 - byte)[:, None, :]).reshape(k, n).astype(np.float32)
    by_word = np.ascontiguousarray(scaled.reshape(k // 512, 128, 4, n).transpose(0, 1, 3, 2))
    if fmt == "e4m3":
        words = by_word.astype(ml_dtypes.float8_e4m3fn).view(np.uint8)
    else:
        c = by_word.astype(ml_dtypes.float4_e2m1fn).view(np.uint8) & 0xF
        words = (c[..., 0::2] | (c[..., 1::2] << 4)).reshape(k // 512, 128, 2 * n)
    return np.ascontiguousarray(words), np.ascontiguousarray(byte.astype(np.uint8).reshape(k // 512, 16, n))


def unpack_weight(words, scales, fmt):
    g, _, n = scales.shape
    words = np.ascontiguousarray(words).reshape(g, 128, n, -1)
    if fmt == "e4m3":
        vals = words.view(ml_dtypes.float8_e4m3fn).astype(np.float64)
    else:
        nib = np.empty((g, 128, n, 4), np.uint8)
        nib[..., 0::2] = words & 0xF
        nib[..., 1::2] = words >> 4
        vals = E2M1[nib]
    vals = vals * np.repeat(np.exp2(scales.astype(np.float64) - 127.0), 8, axis=1)[..., None]
    return vals.transpose(0, 1, 3, 2).reshape(g * 512, n)


def sigmoid(v):
    return 1.0 / (1.0 + np.exp(-v))


D, K, T, U, I, Q = 512, 512, 1024, 1024, 512, 128


def setup_inputs():
    n = np.random.standard_normal
    idx = np.stack([np.random.permutation(T)[:I] for _ in range(8)])
    idx2 = np.stack([np.random.permutation(U)[:I] for _ in range(8)])
    idx3 = np.stack([np.random.permutation(T)[:I] for _ in range(8)])
    idx4 = np.stack([np.random.permutation(T)[:I] for _ in range(8)])
    fd = mx_kscale(D)
    fk = mx_kscale(K)
    wqp = pack_weight(n((D, K)) * 1.0 / np.sqrt(D) * fd[:, None] * fk, "e4m3")
    keysp = pack_weight(n((K, T)) * 1.0 / np.sqrt(K) / fk[:, None], "e2m1")
    notesp = pack_weight(n((D, U)) * 1.0 / np.sqrt(D) * fd[:, None], "e4m3")
    return {
        "states": (n((D, Q)) * 0.95 / fd[:, None]).astype(np.float32),
        "wq_words": wqp[0],
        "wq_scales": wqp[1],
        "keys_words": keysp[0],
        "keys_scales": keysp[1],
        "notes_words": notesp[0],
        "notes_scales": notesp[1],
        "thr": (np.random.uniform(-0.6, 0.6, (Q, 1))).astype(np.float32),
        "slope": (np.random.uniform(1.0, 3.0, (Q, 1))).astype(np.float32),
        "offs": striped8(idx),
        "offs2": striped8(idx2),
        "offs3": striped8(idx3),
        "offs4": striped8(idx4),
    }


def reference(states, wq_words, wq_scales, keys_words, keys_scales, notes_words, notes_scales, thr, slope, offs, offs2, offs3, offs4):
    idx = unstriped8(offs)
    idx2 = unstriped8(offs2)
    idx3 = unstriped8(offs3)
    idx4 = unstriped8(offs4)
    wqu = unpack_weight(wq_words, wq_scales, "e4m3")
    keysu = unpack_weight(keys_words, keys_scales, "e2m1")
    notesu = unpack_weight(notes_words, notes_scales, "e4m3")
    statesq = mxq(f64(states), 0, "e4m3")
    qv = wqu.T @ statesq
    qvq = mxq(qv, 0, "e4m3")
    a = qvq.T @ keysu
    b = statesq.T @ notesu
    s2 = sigmoid(pick8(b, idx2, 16) * f64(slope) + f64(thr))
    f1 = np.zeros((Q, T))
    f1[np.arange(Q)[:, None], idx[np.arange(Q) % 128 // 16]] = s2
    cc = a - f1 * 2.0
    y = np.maximum(pick8(cc, idx3, 16), pick8(cc, idx4, 16))
    return y

@@ -1,0 +1,149 @@
+from contextlib import ExitStack
+
+import concourse.mybir as mybir
+from concourse.masks import make_identity
+
+D, K, T, U, I, Q = 512, 512, 1024, 1024, 512, 128
+FLOPS = 2 * Q * (D * K + K * T + D * U)
+
+F32 = mybir.dt.float32
+BF16 = mybir.dt.bfloat16
+I32 = mybir.dt.int32
+U32 = mybir.dt.uint32
+U16 = mybir.dt.uint16
+U8 = mybir.dt.uint8
+FP8X4 = mybir.dt.float8_e4m3fn_x4
+FP4X4 = mybir.dt.float4_e2m1fn_x4
+ACT = mybir.ActivationFunctionType
+ALU = mybir.AluOpType
+
+P = 128
+PACK = 4
+HALF = I // 2
+HCOL = HALF // 16
+B_PIECE = 256
+A_PIECE = 512
+
+
+def load_scale_rows(queue, plane, scales):
+    for quad in range(4):
+        queue.dma_start(
+            out=plane[32 * quad : 32 * quad + 4, :].bitcast(I32),
+            in_=scales[0, 4 * quad : 4 * quad + 4, :].bitcast(I32),
+        )
+
+
+def tile_attend_guarded_madeside_kernel(
+    tc, states, wq_words, wq_scales, keys_words, keys_scales, notes_words, notes_scales,
+    thr, slope, offs, offs2, offs3, offs4, out,
+):
+    nc = tc.nc
+    with ExitStack() as ctx:
+        sb = ctx.enter_context(tc.tile_pool(name="sb", bufs=1))
+        ps = ctx.enter_context(tc.psum_pool(name="ps", bufs=1))
+
+        notes_plane = sb.tile([P, U], U8, align_bytes=64)
+        wq_plane = sb.tile([P, K], U8, align_bytes=64)
+        keys_plane = sb.tile([P, T], U8, align_bytes=64)
+        f1 = sb.tile([P, T], F32)
+        nc.vector.memset(notes_plane[:].bitcast(I32), 0)
+        nc.vector.memset(wq_plane[:].bitcast(I32), 0)
+        nc.vector.memset(keys_plane[:].bitcast(I32), 0)
+        nc.vector.memset(f1[:], 0.0)
+
+        thr_sb = sb.tile([P, 1], F32)
+        slope_sb = sb.tile([P, 1], F32)
+        ident = sb.tile([P, P], F32)
+        make_identity(nc, ident[:])
+
+        raw = sb.tile([P, PACK, Q], F32)
+        nc.sync.dma_start(out=raw[:], in_=states.rearrange("(p j) q -> p j q", j=PACK))
+        list2 = sb.tile([P, I // 16], U16)
+        nc.sync.dma_start(list2[:], offs2)
+        load_scale_rows(nc.sync, notes_plane, notes_scales)
+        notes_sb = sb.tile([P, U], U32, align_bytes=64)
+        nc.sync.dma_start(out=notes_sb[:].bitcast(I32), in_=notes_words[0].rearrange("p n t -> p (n t)").bitcast(I32))
+        wq_sb = sb.tile([P, K], U32, align_bytes=64)
+        nc.sync.dma_start(out=wq_sb[:].bitcast(I32), in_=wq_words[0].rearrange("p n t -> p (n t)").bitcast(I32))
+        load_scale_rows(nc.sync, wq_plane, wq_scales)
+        nc.sync.dma_start(out=thr_sb[:], in_=thr)
+        nc.sync.dma_start(out=slope_sb[:], in_=slope)
+        list1 = sb.tile([P, I // 16], U16)
+        nc.sync.dma_start(list1[:], offs)
+        keys_sb = sb.tile([P, 2 * T], U8, align_bytes=64)
+        nc.sync.dma_start(out=keys_sb[:].bitcast(I32), in_=keys_words[0].bitcast(I32))
+        load_scale_rows(nc.sync, keys_plane, keys_scales)
+        list3 = sb.tile([P, I // 16], U16)
+        nc.sync.dma_start(list3[:], offs3)
+        list4 = sb.tile([P, I // 16], U16)
+        nc.sync.dma_start(list4[:], offs4)
+
+        st_bf = sb.tile([P, Q, PACK], BF16, align_bytes=64)
+        nc.vector.tensor_copy(out=st_bf[:], in_=raw[:].rearrange("p j q -> p q j"))
+        st_codes = sb.tile([P, Q], U32, align_bytes=64)
+        st_plane = sb.tile([P, Q], U8, align_bytes=64)
+        nc.vector.quantize_mx(out=st_codes[:].bitcast(FP8X4), scales=st_plane[:], in_=st_bf[:].rearrange("p q j -> p (q j)"))
+
+        b_sb = sb.tile([P, U], F32)
+        for n in range(U // B_PIECE):
+            bank = ps.tile([P, B_PIECE], F32, name="b%d" % n)
+            cols = slice(n * B_PIECE, (n + 1) * B_PIECE)
+            nc.tensor.matmul_mx(
+                out=bank[:], lhsT=st_codes[:].bitcast(FP8X4), lhsT_scale=st_plane[:],
+                rhs=notes_sb[:, cols].bitcast(FP8X4), rhs_scale=notes_plane[:, cols],
+                start=True, stop=True,
+            )
+            nc.vector.tensor_copy(out=b_sb[:, cols], in_=bank[:])
+
+        qv_ps = ps.tile([P, K], F32)
+        nc.tensor.matmul_mx(
+            out=qv_ps[:], lhsT=st_codes[:].bitcast(FP8X4), lhsT_scale=st_plane[:],
+            rhs=wq_sb[:].bitcast(FP8X4), rhs_scale=wq_plane[:], start=True, stop=True,
+        )
+
+        s2_first = sb.tile([P, HALF], F32)
+        nc.scalar.activation(s2_first[:], b_sb[:].indirect(list2[:, 0:HCOL]), ACT.Sigmoid, bias=thr_sb[:], scale=slope_sb[:])
+
+        qv_rows = sb.tile([P, K], BF16, tag="shared")
+        nc.vector.tensor_copy(
+            out=qv_rows[:].rearrange("q (u p e) -> q u p e", u=2, e=2),
+            in_=qv_ps[:].rearrange("q (p u e) -> q u p e", u=2, e=2),
+        )
+        nc.vector.tensor_copy(f1[:].indirect(list1[:, 0:HCOL]), s2_first[:])
+
+        turned = ps.tile([P, 2, Q], F32)
+        for u in range(2):
+            nc.tensor.transpose(turned[:, u, :], qv_rows[:].bitcast(F32)[:, u * P : (u + 1) * P], ident[:])
+        qv_bf = sb.tile([P, Q * PACK], BF16, align_bytes=64)
+        nc.scalar.copy(
+            out=qv_bf[:].bitcast(F32).rearrange("p (q u) -> p q u", u=2),
+            in_=turned[:].rearrange("p u q -> p q u"),
+        )
+        qv_codes = sb.tile([P, Q], U32, align_bytes=64)
+        qv_plane = sb.tile([P, Q], U8, align_bytes=64)
+        nc.vector.quantize_mx(out=qv_codes[:].bitcast(FP8X4), scales=qv_plane[:], in_=qv_bf[:])
+
+        s2_second = sb.tile([P, HALF], F32, tag="shared")
+        nc.scalar.activation(s2_second[:], b_sb[:].indirect(list2[:, HCOL : 2 * HCOL]), ACT.Sigmoid, bias=thr_sb[:], scale=slope_sb[:])
+        nc.vector.tensor_copy(f1[:].indirect(list1[:, HCOL : 2 * HCOL]), s2_second[:])
+
+        cc = sb.tile([P, T], F32)
+        for n in range(T // A_PIECE):
+            cols = slice(n * A_PIECE, (n + 1) * A_PIECE)
+            bank = ps.tile([P, A_PIECE], F32, name="a%d" % n)
+            nc.tensor.matmul_mx(
+                out=bank[:], lhsT=qv_codes[:].bitcast(FP8X4), lhsT_scale=qv_plane[:],
+                rhs=keys_sb[:, 2 * n * A_PIECE : 2 * (n + 1) * A_PIECE].bitcast(FP4X4), rhs_scale=keys_plane[:, cols],
+                start=True, stop=True,
+            )
+            nc.vector.scalar_tensor_tensor(out=cc[:, cols], in0=f1[:, cols], scalar=-2.0, in1=bank[:], op0=ALU.mult, op1=ALU.add)
+
+        for h in range(2):
+            entries = slice(h * HCOL, (h + 1) * HCOL)
+            at3 = sb.tile([P, HALF], F32, name="at3_%d" % h)
+            at4 = sb.tile([P, HALF], F32, name="at4_%d" % h)
+            best = sb.tile([P, HALF], F32, name="best_%d" % h)
+            nc.vector.tensor_copy(at3[:], cc[:].indirect(list3[:, entries]))
+            nc.scalar.activation(at4[:], cc[:].indirect(list4[:, entries]), ACT.Copy)
+            nc.vector.tensor_tensor(best[:], at3[:], at4[:], ALU.max)
+            nc.sync.dma_start(out=out[:, h * HALF : (h + 1) * HALF], in_=best[:])

@@ -51,6 +51,10 @@ def tile_attend_guarded_madeside_kernel(
         nc.vector.memset(keys_plane[:].bitcast(I32), 0)
         nc.vector.memset(f1[:], 0.0)
 
+        warm_in = sb.tile([P, 1], F32)
+        warm_out = sb.tile([P, 1], F32)
+        nc.gpsimd.memset(warm_in[:], 0.0)
+        nc.scalar.activation(warm_out[:], warm_in[:], ACT.Sigmoid)
         thr_sb = sb.tile([P, 1], F32)
         slope_sb = sb.tile([P, 1], F32)
         ident = sb.tile([P, P], F32)

@@ -57,16 +57,18 @@ def tile_attend_guarded_madeside_kernel(
         nc.scalar.activation(warm_out[:], warm_in[:], ACT.Sigmoid)
         thr_sb = sb.tile([P, 1], F32)
         slope_sb = sb.tile([P, 1], F32)
-        ident = sb.tile([P, P], F32)
-        make_identity(nc, ident[:])
 
         raw = sb.tile([P, PACK, Q], F32)
         nc.sync.dma_start(out=raw[:], in_=states.rearrange("(p j) q -> p j q", j=PACK))
         list2 = sb.tile([P, I // 16], U16)
         nc.sync.dma_start(list2[:], offs2)
         load_scale_rows(nc.sync, notes_plane, notes_scales)
-        notes_sb = sb.tile([P, U], U32, align_bytes=64)
-        nc.sync.dma_start(out=notes_sb[:].bitcast(I32), in_=notes_words[0].rearrange("p n t -> p (n t)").bitcast(I32))
+        notes_flat = notes_words[0].rearrange("p n t -> p (n t)")
+        notes_a = sb.tile([P, U // 2], U32, align_bytes=64)
+        nc.sync.dma_start(out=notes_a[:].bitcast(I32), in_=notes_flat[:, 0 : 2 * U].bitcast(I32))
+        notes_b = sb.tile([P, U // 2], U32, align_bytes=64)
+        nc.sync.dma_start(out=notes_b[:].bitcast(I32), in_=notes_flat[:, 2 * U : 4 * U].bitcast(I32))
+        notes_sb = [notes_a, notes_b]
         wq_sb = sb.tile([P, K], U32, align_bytes=64)
         nc.sync.dma_start(out=wq_sb[:].bitcast(I32), in_=wq_words[0].rearrange("p n t -> p (n t)").bitcast(I32))
         load_scale_rows(nc.sync, wq_plane, wq_scales)
@@ -81,6 +83,8 @@ def tile_attend_guarded_madeside_kernel(
         nc.sync.dma_start(list3[:], offs3)
         list4 = sb.tile([P, I // 16], U16)
         nc.sync.dma_start(list4[:], offs4)
+        ident = sb.tile([P, P], F32)
+        make_identity(nc, ident[:])
 
         st_bf = sb.tile([P, Q, PACK], BF16, align_bytes=64)
         nc.vector.tensor_copy(out=st_bf[:], in_=raw[:].rearrange("p j q -> p q j"))
@@ -89,17 +93,23 @@ def tile_attend_guarded_madeside_kernel(
         nc.vector.quantize_mx(out=st_codes[:].bitcast(FP8X4), scales=st_plane[:], in_=st_bf[:].rearrange("p q j -> p (q j)"))
 
         b_sb = sb.tile([P, U], F32)
-        for n in range(U // B_PIECE):
-            bank = ps.tile([P, B_PIECE], F32, name="b%d" % n)
-            cols = slice(n * B_PIECE, (n + 1) * B_PIECE)
+        at = 0
+        for n, width in enumerate([256,256,256,128,128]):
+            bank = ps.tile([P, width], F32, name="b%d" % n)
+            cols = slice(at, at + width)
+            part, first = divmod(at, U // 2)
             nc.tensor.matmul_mx(
                 out=bank[:], lhsT=st_codes[:].bitcast(FP8X4), lhsT_scale=st_plane[:],
-                rhs=notes_sb[:, cols].bitcast(FP8X4), rhs_scale=notes_plane[:, cols],
+                rhs=notes_sb[part][:, first : first + width].bitcast(FP8X4), rhs_scale=notes_plane[:, cols],
                 start=True, stop=True,
             )
-            nc.vector.tensor_copy(out=b_sb[:, cols], in_=bank[:])
+            if n in [3]:
+                nc.scalar.copy(out=b_sb[:, cols], in_=bank[:])
+            else:
+                nc.vector.tensor_copy(out=b_sb[:, cols], in_=bank[:])
+            at = at + width
 
-        qv_ps = ps.tile([P, K], F32)
+        qv_ps = ps.tile([P, K], F32, tag="qv")
         nc.tensor.matmul_mx(
             out=qv_ps[:], lhsT=st_codes[:].bitcast(FP8X4), lhsT_scale=st_plane[:],
             rhs=wq_sb[:].bitcast(FP8X4), rhs_scale=wq_plane[:], start=True, stop=True,
@@ -107,15 +117,17 @@ def tile_attend_guarded_madeside_kernel(
 
         s2_first = sb.tile([P, HALF], F32)
         nc.scalar.activation(s2_first[:], b_sb[:].indirect(list2[:, 0:HCOL]), ACT.Sigmoid, bias=thr_sb[:], scale=slope_sb[:])
+        s2_second = sb.tile([P, HALF], F32)
+        nc.scalar.activation(s2_second[:], b_sb[:].indirect(list2[:, HCOL : 2 * HCOL]), ACT.Sigmoid, bias=thr_sb[:], scale=slope_sb[:])
 
         qv_rows = sb.tile([P, K], BF16, tag="shared")
         nc.vector.tensor_copy(
             out=qv_rows[:].rearrange("q (u p e) -> q u p e", u=2, e=2),
             in_=qv_ps[:].rearrange("q (p u e) -> q u p e", u=2, e=2),
         )
-        nc.vector.tensor_copy(f1[:].indirect(list1[:, 0:HCOL]), s2_first[:])
+        nc.vector.tensor_tensor(f1[:].indirect(list1[:, 0:HCOL]), s2_first[:], s2_first[:], ALU.add)
 
-        turned = ps.tile([P, 2, Q], F32)
+        turned = ps.tile([P, 2, Q], F32, tag="qv")
         for u in range(2):
             nc.tensor.transpose(turned[:, u, :], qv_rows[:].bitcast(F32)[:, u * P : (u + 1) * P], ident[:])
         qv_bf = sb.tile([P, Q * PACK], BF16, align_bytes=64)
@@ -127,9 +139,9 @@ def tile_attend_guarded_madeside_kernel(
         qv_plane = sb.tile([P, Q], U8, align_bytes=64)
         nc.vector.quantize_mx(out=qv_codes[:].bitcast(FP8X4), scales=qv_plane[:], in_=qv_bf[:])
 
-        s2_second = sb.tile([P, HALF], F32, tag="shared")
-        nc.scalar.activation(s2_second[:], b_sb[:].indirect(list2[:, HCOL : 2 * HCOL]), ACT.Sigmoid, bias=thr_sb[:], scale=slope_sb[:])
-        nc.vector.tensor_copy(f1[:].indirect(list1[:, HCOL : 2 * HCOL]), s2_second[:])
+        twos = sb.tile([P, HALF], F32, tag="shared")
+        nc.gpsimd.memset(twos[:], 2.0)
+        nc.vector.tensor_tensor(f1[:].indirect(list1[:, HCOL : 2 * HCOL]), s2_second[:], twos[:], ALU.mult)
 
         cc = sb.tile([P, T], F32)
         for n in range(T // A_PIECE):
@@ -140,7 +152,7 @@ def tile_attend_guarded_madeside_kernel(
                 rhs=keys_sb[:, 2 * n * A_PIECE : 2 * (n + 1) * A_PIECE].bitcast(FP4X4), rhs_scale=keys_plane[:, cols],
                 start=True, stop=True,
             )
-            nc.vector.scalar_tensor_tensor(out=cc[:, cols], in0=f1[:, cols], scalar=-2.0, in1=bank[:], op0=ALU.mult, op1=ALU.add)
+            nc.vector.tensor_tensor(cc[:, cols], bank[:], f1[:, cols], ALU.subtract)
 
         for h in range(2):
             entries = slice(h * HCOL, (h + 1) * HCOL)

@@ -63,12 +63,8 @@ def tile_attend_guarded_madeside_kernel(
         list2 = sb.tile([P, I // 16], U16)
         nc.sync.dma_start(list2[:], offs2)
         load_scale_rows(nc.sync, notes_plane, notes_scales)
-        notes_flat = notes_words[0].rearrange("p n t -> p (n t)")
-        notes_a = sb.tile([P, U // 2], U32, align_bytes=64)
-        nc.sync.dma_start(out=notes_a[:].bitcast(I32), in_=notes_flat[:, 0 : 2 * U].bitcast(I32))
-        notes_b = sb.tile([P, U // 2], U32, align_bytes=64)
-        nc.sync.dma_start(out=notes_b[:].bitcast(I32), in_=notes_flat[:, 2 * U : 4 * U].bitcast(I32))
-        notes_sb = [notes_a, notes_b]
+        notes_sb = sb.tile([P, U], U32, align_bytes=64)
+        nc.sync.dma_start(out=notes_sb[:].bitcast(I32), in_=notes_words[0].rearrange("p n t -> p (n t)").bitcast(I32))
         wq_sb = sb.tile([P, K], U32, align_bytes=64)
         nc.sync.dma_start(out=wq_sb[:].bitcast(I32), in_=wq_words[0].rearrange("p n t -> p (n t)").bitcast(I32))
         load_scale_rows(nc.sync, wq_plane, wq_scales)
@@ -87,7 +83,9 @@ def tile_attend_guarded_madeside_kernel(
         make_identity(nc, ident[:])
 
         st_bf = sb.tile([P, Q, PACK], BF16, align_bytes=64)
-        nc.vector.tensor_copy(out=st_bf[:], in_=raw[:].rearrange("p j q -> p q j"))
+        raw_qj = raw[:].rearrange("p j q -> p q j")
+        nc.vector.tensor_copy(out=st_bf[:, 0:80, :], in_=raw_qj[:, 0:80, :])
+        nc.scalar.copy(out=st_bf[:, 80:Q, :], in_=raw_qj[:, 80:Q, :])
         st_codes = sb.tile([P, Q], U32, align_bytes=64)
         st_plane = sb.tile([P, Q], U8, align_bytes=64)
         nc.vector.quantize_mx(out=st_codes[:].bitcast(FP8X4), scales=st_plane[:], in_=st_bf[:].rearrange("p q j -> p (q j)"))
@@ -97,10 +95,9 @@ def tile_attend_guarded_madeside_kernel(
         for n, width in enumerate([256,256,256,128,128]):
             bank = ps.tile([P, width], F32, name="b%d" % n)
             cols = slice(at, at + width)
-            part, first = divmod(at, U // 2)
             nc.tensor.matmul_mx(
                 out=bank[:], lhsT=st_codes[:].bitcast(FP8X4), lhsT_scale=st_plane[:],
-                rhs=notes_sb[part][:, first : first + width].bitcast(FP8X4), rhs_scale=notes_plane[:, cols],
+                rhs=notes_sb[:, cols].bitcast(FP8X4), rhs_scale=notes_plane[:, cols],
                 start=True, stop=True,
             )
             if n in [3]:
@@ -152,7 +149,13 @@ def tile_attend_guarded_madeside_kernel(
                 rhs=keys_sb[:, 2 * n * A_PIECE : 2 * (n + 1) * A_PIECE].bitcast(FP4X4), rhs_scale=keys_plane[:, cols],
                 start=True, stop=True,
             )
-            nc.vector.tensor_tensor(cc[:, cols], bank[:], f1[:, cols], ALU.subtract)
+            skip = 288 if n == 0 else 0
+            if skip:
+                a_sb = sb.tile([P, skip], F32)
+                nc.scalar.copy(out=a_sb[:], in_=bank[:, 0:skip])
+                nc.gpsimd.tensor_tensor(cc[:, 0:skip], a_sb[:], f1[:, 0:skip], ALU.subtract)
+            rest = slice(n * A_PIECE + skip, (n + 1) * A_PIECE)
+            nc.vector.tensor_tensor(cc[:, rest], bank[:, skip:A_PIECE], f1[:, rest], ALU.subtract)
 
         for h in range(2):
             entries = slice(h * HCOL, (h + 1) * HCOL)

@@ -20,17 +20,17 @@ ALU = mybir.AluOpType
 P = 128
 PACK = 4
 HALF = I // 2
-HCOL = HALF // 16
-B_PIECE = 256
-A_PIECE = 512
+HALF_COLS = HALF // 16
+BANK = 512
+B_WIDTHS = (256, 256, 256, 128, 128)
+B_ON_SCALAR = 3
+CAST_ON_VECTOR = 80
+CC_ON_GPSIMD = 352
 
 
-def load_scale_rows(queue, plane, scales):
-    for quad in range(4):
-        queue.dma_start(
-            out=plane[32 * quad : 32 * quad + 4, :].bitcast(I32),
-            in_=scales[0, 4 * quad : 4 * quad + 4, :].bitcast(I32),
-        )
+def load_scale_rows(nc, plane, scales):
+    for r in range(4):
+        nc.sync.dma_start(out=plane[r:P:32, :].bitcast(I32), in_=scales[0, r:16:4, :].bitcast(I32))
 
 
 def tile_attend_guarded_madeside_kernel(
@@ -45,11 +45,11 @@ def tile_attend_guarded_madeside_kernel(
         notes_plane = sb.tile([P, U], U8, align_bytes=64)
         wq_plane = sb.tile([P, K], U8, align_bytes=64)
         keys_plane = sb.tile([P, T], U8, align_bytes=64)
-        f1 = sb.tile([P, T], F32)
+        f1_twice = sb.tile([P, T], F32)
         nc.vector.memset(notes_plane[:].bitcast(I32), 0)
         nc.vector.memset(wq_plane[:].bitcast(I32), 0)
         nc.vector.memset(keys_plane[:].bitcast(I32), 0)
-        nc.vector.memset(f1[:], 0.0)
+        nc.vector.memset(f1_twice[:], 0.0)
 
         warm_in = sb.tile([P, 1], F32)
         warm_out = sb.tile([P, 1], F32)
@@ -58,23 +58,27 @@ def tile_attend_guarded_madeside_kernel(
         thr_sb = sb.tile([P, 1], F32)
         slope_sb = sb.tile([P, 1], F32)
 
-        raw = sb.tile([P, PACK, Q], F32)
-        nc.sync.dma_start(out=raw[:], in_=states.rearrange("(p j) q -> p j q", j=PACK))
+        nc.gpsimd.dma_start(out=slope_sb[:], in_=slope)
+        states_sb = sb.tile([P, PACK, Q], F32)
+        nc.sync.dma_start(out=states_sb[:], in_=states.rearrange("(p t) q -> p t q", t=PACK))
         list2 = sb.tile([P, I // 16], U16)
         nc.sync.dma_start(list2[:], offs2)
-        load_scale_rows(nc.sync, notes_plane, notes_scales)
-        notes_sb = sb.tile([P, U], U32, align_bytes=64)
-        nc.sync.dma_start(out=notes_sb[:].bitcast(I32), in_=notes_words[0].rearrange("p n t -> p (n t)").bitcast(I32))
+        load_scale_rows(nc, notes_plane, notes_scales)
+        notes_bytes = notes_words[0].rearrange("p n t -> p (n t)")
+        notes_low = sb.tile([P, U // 2], U32, align_bytes=64)
+        nc.sync.dma_start(out=notes_low[:].bitcast(I32), in_=notes_bytes[:, 0 : 2 * U].bitcast(I32))
+        notes_high = sb.tile([P, U // 2], U32, align_bytes=64)
+        nc.sync.dma_start(out=notes_high[:].bitcast(I32), in_=notes_bytes[:, 2 * U : 4 * U].bitcast(I32))
+        notes_halves = [notes_low, notes_high]
         wq_sb = sb.tile([P, K], U32, align_bytes=64)
         nc.sync.dma_start(out=wq_sb[:].bitcast(I32), in_=wq_words[0].rearrange("p n t -> p (n t)").bitcast(I32))
-        load_scale_rows(nc.sync, wq_plane, wq_scales)
+        load_scale_rows(nc, wq_plane, wq_scales)
         nc.sync.dma_start(out=thr_sb[:], in_=thr)
-        nc.sync.dma_start(out=slope_sb[:], in_=slope)
         list1 = sb.tile([P, I // 16], U16)
         nc.sync.dma_start(list1[:], offs)
         keys_sb = sb.tile([P, 2 * T], U8, align_bytes=64)
         nc.sync.dma_start(out=keys_sb[:].bitcast(I32), in_=keys_words[0].bitcast(I32))
-        load_scale_rows(nc.sync, keys_plane, keys_scales)
+        load_scale_rows(nc, keys_plane, keys_scales)
         list3 = sb.tile([P, I // 16], U16)
         nc.sync.dma_start(list3[:], offs3)
         list4 = sb.tile([P, I // 16], U16)
@@ -82,47 +86,56 @@ def tile_attend_guarded_madeside_kernel(
         ident = sb.tile([P, P], F32)
         make_identity(nc, ident[:])
 
-        st_bf = sb.tile([P, Q, PACK], BF16, align_bytes=64)
-        raw_qj = raw[:].rearrange("p j q -> p q j")
-        nc.vector.tensor_copy(out=st_bf[:, 0:80, :], in_=raw_qj[:, 0:80, :])
-        nc.scalar.copy(out=st_bf[:, 80:Q, :], in_=raw_qj[:, 80:Q, :])
-        st_codes = sb.tile([P, Q], U32, align_bytes=64)
-        st_plane = sb.tile([P, Q], U8, align_bytes=64)
-        nc.vector.quantize_mx(out=st_codes[:].bitcast(FP8X4), scales=st_plane[:], in_=st_bf[:].rearrange("p q j -> p (q j)"))
+        states_bf = sb.tile([P, Q, PACK], BF16, align_bytes=64)
+        states_qt = states_sb[:].rearrange("p t q -> p q t")
+        nc.vector.tensor_copy(out=states_bf[:, 0:CAST_ON_VECTOR, :], in_=states_qt[:, 0:CAST_ON_VECTOR, :])
+        nc.scalar.copy(out=states_bf[:, CAST_ON_VECTOR:Q, :], in_=states_qt[:, CAST_ON_VECTOR:Q, :])
+        states_codes = sb.tile([P, Q], U32, align_bytes=64)
+        states_plane = sb.tile([P, Q], U8, align_bytes=64)
+        nc.vector.quantize_mx(
+            out=states_codes[:].bitcast(FP8X4), scales=states_plane[:], in_=states_bf[:].rearrange("p q t -> p (q t)")
+        )
 
         b_sb = sb.tile([P, U], F32)
-        at = 0
-        for n, width in enumerate([256,256,256,128,128]):
-            bank = ps.tile([P, width], F32, name="b%d" % n)
-            cols = slice(at, at + width)
+        start = 0
+        for piece, width in enumerate(B_WIDTHS):
+            b_bank = ps.tile([P, width], F32, name="b%d" % piece)
+            cols = slice(start, start + width)
+            which, first = divmod(start, U // 2)
             nc.tensor.matmul_mx(
-                out=bank[:], lhsT=st_codes[:].bitcast(FP8X4), lhsT_scale=st_plane[:],
-                rhs=notes_sb[:, cols].bitcast(FP8X4), rhs_scale=notes_plane[:, cols],
+                out=b_bank[:], lhsT=states_codes[:].bitcast(FP8X4), lhsT_scale=states_plane[:],
+                rhs=notes_halves[which][:, first : first + width].bitcast(FP8X4), rhs_scale=notes_plane[:, cols],
                 start=True, stop=True,
             )
-            if n in [3]:
-                nc.scalar.copy(out=b_sb[:, cols], in_=bank[:])
+            if piece == B_ON_SCALAR:
+                nc.scalar.copy(out=b_sb[:, cols], in_=b_bank[:])
             else:
-                nc.vector.tensor_copy(out=b_sb[:, cols], in_=bank[:])
-            at = at + width
+                nc.vector.tensor_copy(out=b_sb[:, cols], in_=b_bank[:])
+            start = start + width
 
-        qv_ps = ps.tile([P, K], F32, tag="qv")
+        qv_bank = ps.tile([P, K], F32, tag="qv")
         nc.tensor.matmul_mx(
-            out=qv_ps[:], lhsT=st_codes[:].bitcast(FP8X4), lhsT_scale=st_plane[:],
+            out=qv_bank[:], lhsT=states_codes[:].bitcast(FP8X4), lhsT_scale=states_plane[:],
             rhs=wq_sb[:].bitcast(FP8X4), rhs_scale=wq_plane[:], start=True, stop=True,
         )
 
+        first_half = slice(0, HALF_COLS)
+        second_half = slice(HALF_COLS, 2 * HALF_COLS)
         s2_first = sb.tile([P, HALF], F32)
-        nc.scalar.activation(s2_first[:], b_sb[:].indirect(list2[:, 0:HCOL]), ACT.Sigmoid, bias=thr_sb[:], scale=slope_sb[:])
+        nc.scalar.activation(
+            s2_first[:], b_sb[:].indirect(list2[:, first_half]), ACT.Sigmoid, bias=thr_sb[:], scale=slope_sb[:]
+        )
         s2_second = sb.tile([P, HALF], F32)
-        nc.scalar.activation(s2_second[:], b_sb[:].indirect(list2[:, HCOL : 2 * HCOL]), ACT.Sigmoid, bias=thr_sb[:], scale=slope_sb[:])
+        nc.scalar.activation(
+            s2_second[:], b_sb[:].indirect(list2[:, second_half]), ACT.Sigmoid, bias=thr_sb[:], scale=slope_sb[:]
+        )
 
-        qv_rows = sb.tile([P, K], BF16, tag="shared")
+        qv_rows = sb.tile([P, K], BF16, tag="reused")
         nc.vector.tensor_copy(
             out=qv_rows[:].rearrange("q (u p e) -> q u p e", u=2, e=2),
-            in_=qv_ps[:].rearrange("q (p u e) -> q u p e", u=2, e=2),
+            in_=qv_bank[:].rearrange("q (p u e) -> q u p e", u=2, e=2),
         )
-        nc.vector.tensor_tensor(f1[:].indirect(list1[:, 0:HCOL]), s2_first[:], s2_first[:], ALU.add)
+        nc.vector.tensor_tensor(f1_twice[:].indirect(list1[:, first_half]), s2_first[:], s2_first[:], ALU.add)
 
         turned = ps.tile([P, 2, Q], F32, tag="qv")
         for u in range(2):
@@ -136,33 +149,33 @@ def tile_attend_guarded_madeside_kernel(
         qv_plane = sb.tile([P, Q], U8, align_bytes=64)
         nc.vector.quantize_mx(out=qv_codes[:].bitcast(FP8X4), scales=qv_plane[:], in_=qv_bf[:])
 
-        twos = sb.tile([P, HALF], F32, tag="shared")
-        nc.gpsimd.memset(twos[:], 2.0)
-        nc.vector.tensor_tensor(f1[:].indirect(list1[:, HCOL : 2 * HCOL]), s2_second[:], twos[:], ALU.mult)
+        s2_second_twice = sb.tile([P, HALF], F32, tag="reused")
+        nc.scalar.activation(s2_second_twice[:], s2_second[:], ACT.Copy, scale=2.0)
+        nc.vector.tensor_copy(f1_twice[:].indirect(list1[:, second_half]), s2_second_twice[:])
 
         cc = sb.tile([P, T], F32)
-        for n in range(T // A_PIECE):
-            cols = slice(n * A_PIECE, (n + 1) * A_PIECE)
-            bank = ps.tile([P, A_PIECE], F32, name="a%d" % n)
+        for piece in range(T // BANK):
+            a_bank = ps.tile([P, BANK], F32, name="a%d" % piece)
             nc.tensor.matmul_mx(
-                out=bank[:], lhsT=qv_codes[:].bitcast(FP8X4), lhsT_scale=qv_plane[:],
-                rhs=keys_sb[:, 2 * n * A_PIECE : 2 * (n + 1) * A_PIECE].bitcast(FP4X4), rhs_scale=keys_plane[:, cols],
+                out=a_bank[:], lhsT=qv_codes[:].bitcast(FP8X4), lhsT_scale=qv_plane[:],
+                rhs=keys_sb[:, 2 * piece * BANK : 2 * (piece + 1) * BANK].bitcast(FP4X4),
+                rhs_scale=keys_plane[:, piece * BANK : (piece + 1) * BANK],
                 start=True, stop=True,
             )
-            skip = 288 if n == 0 else 0
-            if skip:
-                a_sb = sb.tile([P, skip], F32)
-                nc.scalar.copy(out=a_sb[:], in_=bank[:, 0:skip])
-                nc.gpsimd.tensor_tensor(cc[:, 0:skip], a_sb[:], f1[:, 0:skip], ALU.subtract)
-            rest = slice(n * A_PIECE + skip, (n + 1) * A_PIECE)
-            nc.vector.tensor_tensor(cc[:, rest], bank[:, skip:A_PIECE], f1[:, rest], ALU.subtract)
+            given = 0
+            if piece == 0:
+                given = CC_ON_GPSIMD
+                a_sb = sb.tile([P, given], F32)
+                nc.scalar.copy(out=a_sb[:], in_=a_bank[:, 0:given])
+                nc.gpsimd.tensor_tensor(cc[:, 0:given], a_sb[:], f1_twice[:, 0:given], ALU.subtract)
+            rest = slice(piece * BANK + given, (piece + 1) * BANK)
+            nc.vector.tensor_tensor(cc[:, rest], a_bank[:, given:BANK], f1_twice[:, rest], ALU.subtract)
 
-        for h in range(2):
-            entries = slice(h * HCOL, (h + 1) * HCOL)
-            at3 = sb.tile([P, HALF], F32, name="at3_%d" % h)
-            at4 = sb.tile([P, HALF], F32, name="at4_%d" % h)
-            best = sb.tile([P, HALF], F32, name="best_%d" % h)
+        for half, entries in enumerate((first_half, second_half)):
+            at3 = sb.tile([P, HALF], F32, name="at3_%d" % half)
+            at4 = sb.tile([P, HALF], F32, name="at4_%d" % half)
+            larger = sb.tile([P, HALF], F32, name="larger_%d" % half)
             nc.vector.tensor_copy(at3[:], cc[:].indirect(list3[:, entries]))
             nc.scalar.activation(at4[:], cc[:].indirect(list4[:, entries]), ACT.Copy)
-            nc.vector.tensor_tensor(best[:], at3[:], at4[:], ALU.max)
-            nc.sync.dma_start(out=out[:, h * HALF : (h + 1) * HALF], in_=best[:])
+            nc.vector.tensor_tensor(larger[:], at3[:], at4[:], ALU.max)
+            nc.sync.dma_start(out=out[:, half * HALF : (half + 1) * HALF], in_=larger[:])

from contextlib import ExitStack

import concourse.mybir as mybir
from concourse.masks import make_identity

D, K, T, U, I, Q = 512, 512, 1024, 1024, 512, 128
FLOPS = 2 * Q * (D * K + K * T + D * U)

F32 = mybir.dt.float32
BF16 = mybir.dt.bfloat16
I32 = mybir.dt.int32
U32 = mybir.dt.uint32
U16 = mybir.dt.uint16
U8 = mybir.dt.uint8
FP8X4 = mybir.dt.float8_e4m3fn_x4
FP4X4 = mybir.dt.float4_e2m1fn_x4
ACT = mybir.ActivationFunctionType
ALU = mybir.AluOpType

P = 128
PACK = 4
HALF = I // 2
HALF_COLS = HALF // 16
BANK = 512
B_WIDTHS = (256, 256, 256, 128, 128)
B_ON_SCALAR = 3
CAST_ON_VECTOR = 80
CC_ON_GPSIMD = 352


def load_scale_rows(nc, plane, scales):
    for r in range(4):
        nc.sync.dma_start(out=plane[r:P:32, :].bitcast(I32), in_=scales[0, r:16:4, :].bitcast(I32))


def tile_attend_guarded_madeside_kernel(
    tc, states, wq_words, wq_scales, keys_words, keys_scales, notes_words, notes_scales,
    thr, slope, offs, offs2, offs3, offs4, out,
):
    nc = tc.nc
    with ExitStack() as ctx:
        sb = ctx.enter_context(tc.tile_pool(name="sb", bufs=1))
        ps = ctx.enter_context(tc.psum_pool(name="ps", bufs=1))

        notes_plane = sb.tile([P, U], U8, align_bytes=64)
        wq_plane = sb.tile([P, K], U8, align_bytes=64)
        keys_plane = sb.tile([P, T], U8, align_bytes=64)
        f1_twice = sb.tile([P, T], F32)
        nc.vector.memset(notes_plane[:].bitcast(I32), 0)
        nc.vector.memset(wq_plane[:].bitcast(I32), 0)
        nc.vector.memset(keys_plane[:].bitcast(I32), 0)
        nc.vector.memset(f1_twice[:], 0.0)

        warm_in = sb.tile([P, 1], F32)
        warm_out = sb.tile([P, 1], F32)
        nc.gpsimd.memset(warm_in[:], 0.0)
        nc.scalar.activation(warm_out[:], warm_in[:], ACT.Sigmoid)
        thr_sb = sb.tile([P, 1], F32)
        slope_sb = sb.tile([P, 1], F32)

        nc.gpsimd.dma_start(out=slope_sb[:], in_=slope)
        states_sb = sb.tile([P, PACK, Q], F32)
        nc.sync.dma_start(out=states_sb[:], in_=states.rearrange("(p t) q -> p t q", t=PACK))
        list2 = sb.tile([P, I // 16], U16)
        nc.sync.dma_start(list2[:], offs2)
        load_scale_rows(nc, notes_plane, notes_scales)
        notes_bytes = notes_words[0].rearrange("p n t -> p (n t)")
        notes_low = sb.tile([P, U // 2], U32, align_bytes=64)
        nc.sync.dma_start(out=notes_low[:].bitcast(I32), in_=notes_bytes[:, 0 : 2 * U].bitcast(I32))
        notes_high = sb.tile([P, U // 2], U32, align_bytes=64)
        nc.sync.dma_start(out=notes_high[:].bitcast(I32), in_=notes_bytes[:, 2 * U : 4 * U].bitcast(I32))
        notes_halves = [notes_low, notes_high]
        wq_sb = sb.tile([P, K], U32, align_bytes=64)
        nc.sync.dma_start(out=wq_sb[:].bitcast(I32), in_=wq_words[0].rearrange("p n t -> p (n t)").bitcast(I32))
        load_scale_rows(nc, wq_plane, wq_scales)
        nc.sync.dma_start(out=thr_sb[:], in_=thr)
        list1 = sb.tile([P, I // 16], U16)
        nc.sync.dma_start(list1[:], offs)
        keys_sb = sb.tile([P, 2 * T], U8, align_bytes=64)
        nc.sync.dma_start(out=keys_sb[:].bitcast(I32), in_=keys_words[0].bitcast(I32))
        load_scale_rows(nc, keys_plane, keys_scales)
        list3 = sb.tile([P, I // 16], U16)
        nc.sync.dma_start(list3[:], offs3)
        list4 = sb.tile([P, I // 16], U16)
        nc.sync.dma_start(list4[:], offs4)
        ident = sb.tile([P, P], F32)
        make_identity(nc, ident[:])

        states_bf = sb.tile([P, Q, PACK], BF16, align_bytes=64)
        states_qt = states_sb[:].rearrange("p t q -> p q t")
        nc.vector.tensor_copy(out=states_bf[:, 0:CAST_ON_VECTOR, :], in_=states_qt[:, 0:CAST_ON_VECTOR, :])
        nc.scalar.copy(out=states_bf[:, CAST_ON_VECTOR:Q, :], in_=states_qt[:, CAST_ON_VECTOR:Q, :])
        states_codes = sb.tile([P, Q], U32, align_bytes=64)
        states_plane = sb.tile([P, Q], U8, align_bytes=64)
        nc.vector.quantize_mx(
            out=states_codes[:].bitcast(FP8X4), scales=states_plane[:], in_=states_bf[:].rearrange("p q t -> p (q t)")
        )

        b_sb = sb.tile([P, U], F32)
        start = 0
        for piece, width in enumerate(B_WIDTHS):
            b_bank = ps.tile([P, width], F32, name="b%d" % piece)
            cols = slice(start, start + width)
            which, first = divmod(start, U // 2)
            nc.tensor.matmul_mx(
                out=b_bank[:], lhsT=states_codes[:].bitcast(FP8X4), lhsT_scale=states_plane[:],
                rhs=notes_halves[which][:, first : first + width].bitcast(FP8X4), rhs_scale=notes_plane[:, cols],
                start=True, stop=True,
            )
            if piece == B_ON_SCALAR:
                nc.scalar.copy(out=b_sb[:, cols], in_=b_bank[:])
            else:
                nc.vector.tensor_copy(out=b_sb[:, cols], in_=b_bank[:])
            start = start + width

        qv_bank = ps.tile([P, K], F32, tag="qv")
        nc.tensor.matmul_mx(
            out=qv_bank[:], lhsT=states_codes[:].bitcast(FP8X4), lhsT_scale=states_plane[:],
            rhs=wq_sb[:].bitcast(FP8X4), rhs_scale=wq_plane[:], start=True, stop=True,
        )

        first_half = slice(0, HALF_COLS)
        second_half = slice(HALF_COLS, 2 * HALF_COLS)
        s2_first = sb.tile([P, HALF], F32)
        nc.scalar.activation(
            s2_first[:], b_sb[:].indirect(list2[:, first_half]), ACT.Sigmoid, bias=thr_sb[:], scale=slope_sb[:]
        )
        s2_second = sb.tile([P, HALF], F32)
        nc.scalar.activation(
            s2_second[:], b_sb[:].indirect(list2[:, second_half]), ACT.Sigmoid, bias=thr_sb[:], scale=slope_sb[:]
        )

        qv_rows = sb.tile([P, K], BF16, tag="reused")
        nc.vector.tensor_copy(
            out=qv_rows[:].rearrange("q (u p e) -> q u p e", u=2, e=2),
            in_=qv_bank[:].rearrange("q (p u e) -> q u p e", u=2, e=2),
        )
        nc.vector.tensor_tensor(f1_twice[:].indirect(list1[:, first_half]), s2_first[:], s2_first[:], ALU.add)

        turned = ps.tile([P, 2, Q], F32, tag="qv")
        for u in range(2):
            nc.tensor.transpose(turned[:, u, :], qv_rows[:].bitcast(F32)[:, u * P : (u + 1) * P], ident[:])
        qv_bf = sb.tile([P, Q * PACK], BF16, align_bytes=64)
        nc.scalar.copy(
            out=qv_bf[:].bitcast(F32).rearrange("p (q u) -> p q u", u=2),
            in_=turned[:].rearrange("p u q -> p q u"),
        )
        qv_codes = sb.tile([P, Q], U32, align_bytes=64)
        qv_plane = sb.tile([P, Q], U8, align_bytes=64)
        nc.vector.quantize_mx(out=qv_codes[:].bitcast(FP8X4), scales=qv_plane[:], in_=qv_bf[:])

        s2_second_twice = sb.tile([P, HALF], F32, tag="reused")
        nc.scalar.activation(s2_second_twice[:], s2_second[:], ACT.Copy, scale=2.0)
        nc.vector.tensor_copy(f1_twice[:].indirect(list1[:, second_half]), s2_second_twice[:])

        cc = sb.tile([P, T], F32)
        for piece in range(T // BANK):
            a_bank = ps.tile([P, BANK], F32, name="a%d" % piece)
            nc.tensor.matmul_mx(
                out=a_bank[:], lhsT=qv_codes[:].bitcast(FP8X4), lhsT_scale=qv_plane[:],
                rhs=keys_sb[:, 2 * piece * BANK : 2 * (piece + 1) * BANK].bitcast(FP4X4),
                rhs_scale=keys_plane[:, piece * BANK : (piece + 1) * BANK],
                start=True, stop=True,
            )
            given = 0
            if piece == 0:
                given = CC_ON_GPSIMD
                a_sb = sb.tile([P, given], F32)
                nc.scalar.copy(out=a_sb[:], in_=a_bank[:, 0:given])
                nc.gpsimd.tensor_tensor(cc[:, 0:given], a_sb[:], f1_twice[:, 0:given], ALU.subtract)
            rest = slice(piece * BANK + given, (piece + 1) * BANK)
            nc.vector.tensor_tensor(cc[:, rest], a_bank[:, given:BANK], f1_twice[:, rest], ALU.subtract)

        for half, entries in enumerate((first_half, second_half)):
            at3 = sb.tile([P, HALF], F32, name="at3_%d" % half)
            at4 = sb.tile([P, HALF], F32, name="at4_%d" % half)
            larger = sb.tile([P, HALF], F32, name="larger_%d" % half)
            nc.vector.tensor_copy(at3[:], cc[:].indirect(list3[:, entries]))
            nc.scalar.activation(at4[:], cc[:].indirect(list4[:, entries]), ACT.Copy)
            nc.vector.tensor_tensor(larger[:], at3[:], at4[:], ALU.max)
            nc.sync.dma_start(out=out[:, half * HALF : (half + 1) * HALF], in_=larger[:])
